import numpy as np
import ml_dtypes


def mxq(x, axis, fmt="e4m3"):
    dtype, down = {"e4m3": (ml_dtypes.float8_e4m3fn, 7), "e5m2": (ml_dtypes.float8_e5m2, 14)}[fmt]
    v = np.moveaxis(np.asarray(x, np.float32).astype(ml_dtypes.bfloat16).astype(np.float64), axis, -1)
    blocks = v.reshape(v.shape[:-1] + (-1, 32))
    amax = np.abs(blocks).max(-1, keepdims=True)
    byte = np.maximum(np.where(amax > 0, np.frexp(amax)[1] - 1 + 127, 0) - down, 1)
    scale = np.exp2(byte - 127.0)
    codes = (blocks / scale).astype(np.float32).astype(dtype).astype(np.float64)
    return np.moveaxis((codes * scale).reshape(v.shape), -1, axis)


WIDE = False


def mx_kscale(k):
    if not WIDE:
        return np.ones(k)
    levels = np.array([10, -10, 5, -5, 0])
    if k % 512:
        return np.exp2(np.random.permutation(np.resize(levels, k // 32))).repeat(32)
    a = np.empty((k // 512, 16))
    for p in range(k // 512):
        a[p, :8] = np.random.permutation(np.resize(levels, 8))
        for g in range(8):
            far = levels[np.abs(levels - a[p, g]) >= 10]
            a[p, g + 8] = far[np.random.randint(len(far))]
    return np.exp2(a.ravel()).repeat(32)


def f64(x):
    return np.asarray(x).astype(np.float64)


def striped(idx):
    return np.tile(np.asarray(idx).reshape(-1, 16).T, (8, 1)).astype(np.uint16)


def unstriped(offs):
    return offs[:16].T.reshape(-1).astype(np.int64)


E2M1 = np.array([0.0, 0.5, 1.0, 1.5, 2.0, 3.0, 4.0, 6.0, -0.0, -0.5, -1.0, -1.5, -2.0, -3.0, -4.0, -6.0])


def pack_weight(w, fmt):
    k, n = w.shape
    w = f64(np.asarray(w, np.float32).astype(ml_dtypes.bfloat16)).reshape(k // 32, 32, n)
    amax = np.abs(w).max(1)
    if fmt == "e4m3":
        byte = np.frexp(amax)[1] - 1 + 127 - 7
    else:
        mant, ex = np.frexp(amax / 6.0)
        byte = np.where(mant > 0.5, ex, ex - 1) + 127
    byte = np.clip(np.where(amax > 0, byte, 1), 1, 254)
    scaled = (w * np.exp2(127.0 - byte)[:, None, :]).reshape(k, n).astype(np.float32)
    by_word = np.ascontiguousarray(scaled.reshape(k // 512, 128, 4, n).transpose(0, 1, 3, 2))
    if fmt == "e4m3":
        words = by_word.astype(ml_dtypes.float8_e4m3fn).view(np.uint8)
    else:
        c = by_word.astype(ml_dtypes.float4_e2m1fn).view(np.uint8) & 0xF
        words = (c[..., 0::2] | (c[..., 1::2] << 4)).reshape(k // 512, 128, 2 * n)
    return np.ascontiguousarray(words), np.ascontiguousarray(byte.astype(np.uint8).reshape(k // 512, 16, n))


def unpack_weight(words, scales, fmt):
    g, _, n = scales.shape
    words = np.ascontiguousarray(words).reshape(g, 128, n, -1)
    if fmt == "e4m3":
        vals = words.view(ml_dtypes.float8_e4m3fn).astype(np.float64)
    else:
        nib = np.empty((g, 128, n, 4), np.uint8)
        nib[..., 0::2] = words & 0xF
        nib[..., 1::2] = words >> 4
        vals = E2M1[nib]
    vals = vals * np.repeat(np.exp2(scales.astype(np.float64) - 127.0), 8, axis=1)[..., None]
    return vals.transpose(0, 1, 3, 2).reshape(g * 512, n)


K, T, J, N = 512, 2048, 1536, 256


def setup_inputs():
    n = np.random.standard_normal
    idx = np.random.permutation(T)[:J]
    fk = mx_kscale(K)
    xqp = pack_weight(n((K, T)) / fk[:, None], "e2m1")
    wap = pack_weight(n((K, N)) * 1 / np.sqrt(K) * fk[:, None], "e2m1")
    wfp = pack_weight(n((K, N)) * 1 / np.sqrt(K) * fk[:, None], "e4m3")
    return {
        "xq_words": xqp[0],
        "xq_scales": xqp[1],
        "wa_words": wap[0],
        "wa_scales": wap[1],
        "xf": (n((K, J)) / fk[:, None]).astype(np.float32),
        "wf_words": wfp[0],
        "wf_scales": wfp[1],
        "fac": (np.random.uniform(0.3, 1.0, (1, J))).astype(np.float32),
        "offs": striped(idx),
    }


def reference(xq_words, xq_scales, wa_words, wa_scales, xf, wf_words, wf_scales, fac, offs):
    idx = unstriped(offs)
    xqu = unpack_weight(xq_words, xq_scales, "e2m1")
    wau = unpack_weight(wa_words, wa_scales, "e2m1")
    wfu = unpack_weight(wf_words, wf_scales, "e4m3")
    z = wau.T @ xqu
    xfq = mxq(f64(xf), 0, "e4m3")
    p = wfu.T @ xfq
    d = f64(fac) * (p - z[:, idx])
    pg = np.zeros((N, T))
    pg[:, idx] = d
    y = z + pg
    return y

@@ -1,0 +1,171 @@
+from contextlib import ExitStack
+
+import concourse.mybir as mybir
+from concourse.masks import make_identity
+
+K, T, J, N = 512, 2048, 1536, 256
+FLOPS = 2 * K * N * (T + J)
+
+F32 = mybir.dt.float32
+BF16 = mybir.dt.bfloat16
+I32 = mybir.dt.int32
+U32 = mybir.dt.uint32
+U16 = mybir.dt.uint16
+U8 = mybir.dt.uint8
+FP8X4 = mybir.dt.float8_e4m3fn_x4
+FP4X4 = mybir.dt.float4_e2m1fn_x4
+ALU = mybir.AluOpType
+
+P = 128
+PACK = 4
+BANK = 512
+GROUP = 16
+CHUNKS = ((0, 256), (256, 512), (512, 1024), (1024, 1536))
+SECOND = ((0, 512), (512, 1536))
+TAIL = ((0, 256), (256, 768), (768, 1280), (1280, 1792), (1792, 2048))
+
+
+def tile_list_token_overrides_kernel(tc, xq_words, xq_scales, wa_words, wa_scales, xf, wf_words, wf_scales, fac, offs, out):
+    nc = tc.nc
+    with ExitStack() as ctx:
+        keep = ctx.enter_context(tc.tile_pool(name="keep", bufs=1))
+        ring = ctx.enter_context(tc.tile_pool(name="ring", bufs=2))
+        psum = ctx.enter_context(tc.psum_pool(name="psum", bufs=1))
+
+        offsets = keep.tile([P, J // GROUP], U16, name="offsets")
+        xq_c = keep.tile([P, 2 * T], U8, name="xq_c", align_bytes=64)
+        xq_s = keep.tile([P, T], U8, name="xq_s", align_bytes=64)
+        wa_c = keep.tile([P, 2 * N], U8, name="wa_c", align_bytes=64)
+        wa_s = keep.tile([P, N], U8, name="wa_s", align_bytes=64)
+        wf_c = keep.tile([P, N], U32, name="wf_c", align_bytes=64)
+        wf_s = keep.tile([P, N], U8, name="wf_s", align_bytes=64)
+        fac_col = keep.tile([P, J // BANK, PACK], F32, name="fac_col")
+        neg_col = keep.tile([P, J // BANK, PACK], F32, name="neg_col")
+        neg_fac = keep.tile([P, J], F32, name="neg_fac")
+        ident = keep.tile([P, P], F32, name="ident")
+        z = [keep.tile([P, T], F32, name="z%d" % b) for b in range(2)]
+        page = [keep.tile([P, T], F32, name="page%d" % b) for b in range(2)]
+        p_sb = [keep.tile([P, J], F32, name="p%d" % b) for b in range(2)]
+        diff = keep.tile([P, J], F32, name="diff")
+        raw = [keep.tile([P, PACK, hi - lo], F32, name="raw%d" % lo) for lo, hi in CHUNKS]
+
+        def load_scale_rows(queue, plane, rows, q):
+            queue.dma_start(out=plane[32 * q : 32 * q + 4, :].bitcast(I32), in_=rows[0, 4 * q : 4 * q + 4, :].bitcast(I32))
+
+        nc.gpsimd.memset(wa_s[:].bitcast(I32), 0)
+        nc.vector.memset(xq_s[:].bitcast(I32), 0)
+        nc.vector.memset(wf_s[:].bitcast(I32), 0)
+        nc.sync.dma_start(out=xq_c[:].bitcast(I32), in_=xq_words[0].bitcast(I32))
+        for q in range(4):
+            load_scale_rows(nc.sync, xq_s, xq_scales, q)
+        nc.sync.dma_start(out=wa_c[:].bitcast(I32), in_=wa_words[0].bitcast(I32))
+        for q in range(4):
+            load_scale_rows(nc.gpsimd if q < 2 else nc.sync, wa_s, wa_scales, q)
+        xf_rows = xf.rearrange("(p t) j -> p t j", t=PACK)
+        nc.sync.dma_start(out=raw[0][:], in_=xf_rows[:, :, CHUNKS[0][0] : CHUNKS[0][1]])
+        nc.sync.dma_start(out=wf_c[:].bitcast(I32), in_=wf_words[0].rearrange("p n t -> p (n t)").bitcast(I32))
+        for q in range(4):
+            load_scale_rows(nc.sync, wf_s, wf_scales, q)
+        nc.sync.dma_start(out=offsets[:], in_=offs)
+        nc.sync.dma_start(out=fac_col[:], in_=fac.rearrange("o (c n m) -> n (o c) m", n=P, m=PACK))
+        for c in range(1, len(CHUNKS)):
+            nc.sync.dma_start(out=raw[c][:], in_=xf_rows[:, :, CHUNKS[c][0] : CHUNKS[c][1]])
+
+        for b in range(2):
+            nc.vector.memset(page[b][:], 0.0)
+        make_identity(nc, ident[:])
+
+        def z_block(b, on_vector):
+            for c in range(T // BANK):
+                acc = psum.tile([P, BANK], F32, name="wide", tag="wide", bufs=4)
+                nc.tensor.matmul_mx(
+                    out=acc[:],
+                    lhsT=wa_c[:, 2 * P * b : 2 * P * (b + 1)].bitcast(FP4X4),
+                    lhsT_scale=wa_s[:, P * b : P * (b + 1)],
+                    rhs=xq_c[:, 2 * BANK * c : 2 * BANK * (c + 1)].bitcast(FP4X4),
+                    rhs_scale=xq_s[:, BANK * c : BANK * (c + 1)],
+                    start=True,
+                    stop=True,
+                )
+                dst = z[b][:, BANK * c : BANK * (c + 1)]
+                if c in on_vector:
+                    nc.vector.tensor_copy(out=dst, in_=acc[:])
+                else:
+                    nc.scalar.copy(out=dst, in_=acc[:])
+
+        def p_chunk(c):
+            lo, hi = CHUNKS[c]
+            w = hi - lo
+            grouped = keep.tile([P, w, PACK], BF16, name="grouped%d" % c, align_bytes=64)
+            codes = keep.tile([P, w], U32, name="codes%d" % c, align_bytes=64)
+            scales = keep.tile([P, w], U8, name="scales%d" % c, align_bytes=64)
+            dst = grouped[:].rearrange("p (g i) t -> p g t i", i=4)
+            src = raw[c][:].rearrange("p t (g i) -> p g t i", i=4)
+            if c == 0:
+                nc.vector.tensor_copy(out=dst, in_=src)
+            else:
+                nc.scalar.copy(out=dst, in_=src)
+            nc.vector.quantize_mx(out=codes[:].bitcast(FP8X4), scales=scales[:], in_=grouped[:].rearrange("p w t -> p (w t)"))
+            for b in range(2):
+                acc = psum.tile([P, BANK], F32, name="prod", tag="prod", bufs=2)
+                nc.tensor.matmul_mx(
+                    out=acc[:, :w],
+                    lhsT=wf_c[:, P * b : P * (b + 1)].bitcast(FP8X4),
+                    lhsT_scale=wf_s[:, P * b : P * (b + 1)],
+                    rhs=codes[:].bitcast(FP8X4),
+                    rhs_scale=scales[:],
+                    start=True,
+                    stop=True,
+                )
+                nc.scalar.copy(out=p_sb[b][:, lo:hi], in_=acc[:, :w])
+
+        def spread_fac(c):
+            acc = psum.tile([P, PACK, P], F32, name="turn", tag="turn", bufs=2)
+            for m in range(PACK):
+                nc.tensor.transpose(acc[:, m, :], neg_col[:, c, m : m + 1].to_broadcast([P, P]), ident[:])
+            nc.scalar.copy(
+                out=neg_fac[:, BANK * c : BANK * (c + 1)].rearrange("p (n m) -> p n m", m=PACK),
+                in_=acc[:].rearrange("p m n -> p n m"),
+            )
+
+        def override(b, lo, hi):
+            listed = offsets[:, lo // GROUP : hi // GROUP]
+            nc.vector.tensor_tensor(diff[:, lo:hi], z[b][:].indirect(listed), p_sb[b][:, lo:hi], ALU.subtract)
+            nc.vector.tensor_tensor(page[b][:].indirect(listed), diff[:, lo:hi], neg_fac[:, lo:hi], ALU.mult)
+
+        z_block(0, (1, 3))
+        nc.gpsimd.tensor_scalar(neg_col[:], fac_col[:], -1.0, 0.0, ALU.mult, ALU.add)
+        z_block(1, (1,))
+        p_chunk(0)
+        spread_fac(0)
+        override(0, *CHUNKS[0])
+        p_chunk(1)
+        override(0, *CHUNKS[1])
+        override(1, *SECOND[0])
+        p_chunk(2)
+        spread_fac(1)
+        override(0, *CHUNKS[2])
+        p_chunk(3)
+        spread_fac(2)
+        override(0, *CHUNKS[3])
+        override(1, *SECOND[1])
+
+        for c in range(T // BANK):
+            summed = psum.tile([P, PACK, P], F32, name="summed", tag="wide", bufs=4)
+            for i in range(PACK):
+                cols = slice(BANK * c + P * i, BANK * c + P * (i + 1))
+                nc.tensor.matmul(summed[:, i, :], z[0][:, cols], ident[:], start=True, stop=False, is_transpose=True)
+                nc.tensor.matmul(summed[:, i, :], page[0][:, cols], ident[:], start=False, stop=True, is_transpose=True)
+            turned = ring.tile([P, PACK, P], F32, name="turned")
+            nc.scalar.copy(out=turned[:], in_=summed[:])
+            back = psum.tile([P, PACK, P], F32, name="back", tag="turn", bufs=2)
+            for i in range(PACK):
+                nc.tensor.transpose(back[:, i, :], turned[:, i, :], ident[:])
+            done = keep.tile([P, BANK], F32, name="done%d" % c)
+            nc.scalar.copy(out=done[:], in_=back[:].rearrange("p i n -> p (i n)"))
+            nc.sync.dma_start(out=out[0:P, BANK * c : BANK * (c + 1)], in_=done[:])
+
+        for lo, hi in TAIL:
+            last = keep.tile([P, hi - lo], F32, name="last%d" % lo)
+            nc.vector.tensor_tensor(last[:], z[1][:, lo:hi], page[1][:, lo:hi], ALU.add)
+            nc.sync.dma_start(out=out[P : 2 * P, lo:hi], in_=last[:])

@@ -21,7 +21,7 @@ PACK = 4
 BANK = 512
 GROUP = 16
 CHUNKS = ((0, 256), (256, 512), (512, 1024), (1024, 1536))
-SECOND = ((0, 512), (512, 1536))
+SECOND = ((0, 256), (256, 512), (512, 768), (768, 1536))
 TAIL = ((0, 256), (256, 768), (768, 1280), (1280, 1792), (1792, 2048))
 
 
@@ -46,38 +46,38 @@ def tile_list_token_overrides_kernel(tc, xq_words, xq_scales, wa_words, wa_scale
         z = [keep.tile([P, T], F32, name="z%d" % b) for b in range(2)]
         page = [keep.tile([P, T], F32, name="page%d" % b) for b in range(2)]
         p_sb = [keep.tile([P, J], F32, name="p%d" % b) for b in range(2)]
-        diff = keep.tile([P, J], F32, name="diff")
         raw = [keep.tile([P, PACK, hi - lo], F32, name="raw%d" % lo) for lo, hi in CHUNKS]
 
         def load_scale_rows(queue, plane, rows, q):
             queue.dma_start(out=plane[32 * q : 32 * q + 4, :].bitcast(I32), in_=rows[0, 4 * q : 4 * q + 4, :].bitcast(I32))
 
-        nc.gpsimd.memset(wa_s[:].bitcast(I32), 0)
-        nc.vector.memset(xq_s[:].bitcast(I32), 0)
-        nc.vector.memset(wf_s[:].bitcast(I32), 0)
-        nc.sync.dma_start(out=xq_c[:].bitcast(I32), in_=xq_words[0].bitcast(I32))
-        for q in range(4):
-            load_scale_rows(nc.sync, xq_s, xq_scales, q)
-        nc.sync.dma_start(out=wa_c[:].bitcast(I32), in_=wa_words[0].bitcast(I32))
-        for q in range(4):
-            load_scale_rows(nc.gpsimd if q < 2 else nc.sync, wa_s, wa_scales, q)
         xf_rows = xf.rearrange("(p t) j -> p t j", t=PACK)
-        nc.sync.dma_start(out=raw[0][:], in_=xf_rows[:, :, CHUNKS[0][0] : CHUNKS[0][1]])
+        load_scale_rows(nc.gpsimd, wa_s, wa_scales, 0)
+        nc.gpsimd.dma_start(out=fac_col[:], in_=fac.rearrange("o (c n m) -> n (o c) m", n=P, m=PACK))
+        load_scale_rows(nc.sync, wa_s, wa_scales, 1)
+        nc.scalar.dma_start(out=wa_c[:].bitcast(I32), in_=wa_words[0].bitcast(I32))
+        nc.sync.dma_start(out=xq_c[:].bitcast(I32), in_=xq_words[0].bitcast(I32))
+        load_scale_rows(nc.scalar, wa_s, wa_scales, 2)
+        for q in range(4):
+            load_scale_rows(nc.scalar if q % 2 else nc.sync, xq_s, xq_scales, q)
+        load_scale_rows(nc.sync, wa_s, wa_scales, 3)
+        for c in range(2):
+            nc.sync.dma_start(out=raw[c][:], in_=xf_rows[:, :, CHUNKS[c][0] : CHUNKS[c][1]])
         nc.sync.dma_start(out=wf_c[:].bitcast(I32), in_=wf_words[0].rearrange("p n t -> p (n t)").bitcast(I32))
         for q in range(4):
             load_scale_rows(nc.sync, wf_s, wf_scales, q)
         nc.sync.dma_start(out=offsets[:], in_=offs)
-        nc.sync.dma_start(out=fac_col[:], in_=fac.rearrange("o (c n m) -> n (o c) m", n=P, m=PACK))
-        for c in range(1, len(CHUNKS)):
+        for c in range(2, len(CHUNKS)):
             nc.sync.dma_start(out=raw[c][:], in_=xf_rows[:, :, CHUNKS[c][0] : CHUNKS[c][1]])
 
-        for b in range(2):
-            nc.vector.memset(page[b][:], 0.0)
+        nc.vector.memset(page[0][:, : T // 2 - 1], 0.0)
+        nc.vector.memset(page[0][:, T // 2 - 1 :], 0.0)
         make_identity(nc, ident[:])
+        nc.gpsimd.memset(page[1][:], 0.0)
 
-        def z_block(b, on_vector):
+        def z_block(b, tag, bufs):
             for c in range(T // BANK):
-                acc = psum.tile([P, BANK], F32, name="wide", tag="wide", bufs=4)
+                acc = psum.tile([P, BANK], F32, name="z_acc", tag=tag, bufs=bufs)
                 nc.tensor.matmul_mx(
                     out=acc[:],
                     lhsT=wa_c[:, 2 * P * b : 2 * P * (b + 1)].bitcast(FP4X4),
@@ -87,37 +87,38 @@ def tile_list_token_overrides_kernel(tc, xq_words, xq_scales, wa_words, wa_scale
                     start=True,
                     stop=True,
                 )
-                dst = z[b][:, BANK * c : BANK * (c + 1)]
-                if c in on_vector:
-                    nc.vector.tensor_copy(out=dst, in_=acc[:])
-                else:
-                    nc.scalar.copy(out=dst, in_=acc[:])
+                nc.scalar.copy(out=z[b][:, BANK * c : BANK * (c + 1)], in_=acc[:])
 
-        def p_chunk(c):
+        def quantise(c):
             lo, hi = CHUNKS[c]
             w = hi - lo
-            grouped = keep.tile([P, w, PACK], BF16, name="grouped%d" % c, align_bytes=64)
+            grouped = keep.tile([P, w, PACK], BF16, name="grouped%d" % c, tag="stage%d" % c, align_bytes=64)
             codes = keep.tile([P, w], U32, name="codes%d" % c, align_bytes=64)
             scales = keep.tile([P, w], U8, name="scales%d" % c, align_bytes=64)
             dst = grouped[:].rearrange("p (g i) t -> p g t i", i=4)
             src = raw[c][:].rearrange("p t (g i) -> p g t i", i=4)
-            if c == 0:
+            if c < 2:
                 nc.vector.tensor_copy(out=dst, in_=src)
             else:
                 nc.scalar.copy(out=dst, in_=src)
             nc.vector.quantize_mx(out=codes[:].bitcast(FP8X4), scales=scales[:], in_=grouped[:].rearrange("p w t -> p (w t)"))
-            for b in range(2):
-                acc = psum.tile([P, BANK], F32, name="prod", tag="prod", bufs=2)
-                nc.tensor.matmul_mx(
-                    out=acc[:, :w],
-                    lhsT=wf_c[:, P * b : P * (b + 1)].bitcast(FP8X4),
-                    lhsT_scale=wf_s[:, P * b : P * (b + 1)],
-                    rhs=codes[:].bitcast(FP8X4),
-                    rhs_scale=scales[:],
-                    start=True,
-                    stop=True,
-                )
-                nc.scalar.copy(out=p_sb[b][:, lo:hi], in_=acc[:, :w])
+            return codes, scales
+
+        def p_block(c, b, operand):
+            lo, hi = CHUNKS[c]
+            w = hi - lo
+            codes, scales = operand
+            acc = psum.tile([P, BANK], F32, name="prod", tag="prod", bufs=2)
+            nc.tensor.matmul_mx(
+                out=acc[:, :w],
+                lhsT=wf_c[:, P * b : P * (b + 1)].bitcast(FP8X4),
+                lhsT_scale=wf_s[:, P * b : P * (b + 1)],
+                rhs=codes[:].bitcast(FP8X4),
+                rhs_scale=scales[:],
+                start=True,
+                stop=True,
+            )
+            nc.scalar.copy(out=p_sb[b][:, lo:hi], in_=acc[:, :w])
 
         def spread_fac(c):
             acc = psum.tile([P, PACK, P], F32, name="turn", tag="turn", bufs=2)
@@ -128,27 +129,32 @@ def tile_list_token_overrides_kernel(tc, xq_words, xq_scales, wa_words, wa_scale
                 in_=acc[:].rearrange("p m n -> p n m"),
             )
 
-        def override(b, lo, hi):
+        def override(b, lo, hi, slot):
             listed = offsets[:, lo // GROUP : hi // GROUP]
-            nc.vector.tensor_tensor(diff[:, lo:hi], z[b][:].indirect(listed), p_sb[b][:, lo:hi], ALU.subtract)
-            nc.vector.tensor_tensor(page[b][:].indirect(listed), diff[:, lo:hi], neg_fac[:, lo:hi], ALU.mult)
+            diff = keep.tile([P, hi - lo], F32, name="diff%d_%d" % (b, lo), tag=slot, align_bytes=64)
+            nc.vector.tensor_tensor(diff[:], z[b][:].indirect(listed), p_sb[b][:, lo:hi], ALU.subtract)
+            nc.vector.tensor_tensor(page[b][:].indirect(listed), diff[:], neg_fac[:, lo:hi], ALU.mult)
 
-        z_block(0, (1, 3))
+        z_block(0, "wide", 4)
+        operands = [quantise(0), quantise(1)]
         nc.gpsimd.tensor_scalar(neg_col[:], fac_col[:], -1.0, 0.0, ALU.mult, ALU.add)
-        z_block(1, (1,))
-        p_chunk(0)
+        p_block(0, 0, operands[0])
         spread_fac(0)
-        override(0, *CHUNKS[0])
-        p_chunk(1)
-        override(0, *CHUNKS[1])
-        override(1, *SECOND[0])
-        p_chunk(2)
-        spread_fac(1)
-        override(0, *CHUNKS[2])
-        p_chunk(3)
-        spread_fac(2)
-        override(0, *CHUNKS[3])
-        override(1, *SECOND[1])
+        p_block(1, 0, operands[1])
+        override(0, *CHUNKS[0], "stage1")
+        override(0, *CHUNKS[1], "diff")
+        z_block(1, "prod", 2)
+        p_block(0, 1, operands[0])
+        p_block(1, 1, operands[1])
+        override(1, *SECOND[0], "stage0")
+        for c in range(2, len(CHUNKS)):
+            spread_fac(c - 1)
+            operand = quantise(c)
+            override(1, *SECOND[c - 1], "stage%d" % c)
+            p_block(c, 0, operand)
+            override(0, *CHUNKS[c], "diff")
+            p_block(c, 1, operand)
+        override(1, *SECOND[-1], "diff")
 
         for c in range(T // BANK):
             summed = psum.tile([P, PACK, P], F32, name="summed", tag="wide", bufs=4)

@@ -21,7 +21,6 @@ PACK = 4
 BANK = 512
 GROUP = 16
 CHUNKS = ((0, 256), (256, 512), (512, 1024), (1024, 1536))
-SECOND = ((0, 256), (256, 512), (512, 768), (768, 1536))
 TAIL = ((0, 256), (256, 768), (768, 1280), (1280, 1792), (1792, 2048))
 
 
@@ -33,7 +32,7 @@ def tile_list_token_overrides_kernel(tc, xq_words, xq_scales, wa_words, wa_scale
         psum = ctx.enter_context(tc.psum_pool(name="psum", bufs=1))
 
         offsets = keep.tile([P, J // GROUP], U16, name="offsets")
-        xq_c = keep.tile([P, 2 * T], U8, name="xq_c", align_bytes=64)
+        xq_c = keep.tile([P, 2 * T], U8, name="xq_c", tag="stage2", align_bytes=64)
         xq_s = keep.tile([P, T], U8, name="xq_s", align_bytes=64)
         wa_c = keep.tile([P, 2 * N], U8, name="wa_c", align_bytes=64)
         wa_s = keep.tile([P, N], U8, name="wa_s", align_bytes=64)
@@ -52,15 +51,15 @@ def tile_list_token_overrides_kernel(tc, xq_words, xq_scales, wa_words, wa_scale
             queue.dma_start(out=plane[32 * q : 32 * q + 4, :].bitcast(I32), in_=rows[0, 4 * q : 4 * q + 4, :].bitcast(I32))
 
         xf_rows = xf.rearrange("(p t) j -> p t j", t=PACK)
-        load_scale_rows(nc.gpsimd, wa_s, wa_scales, 0)
         nc.gpsimd.dma_start(out=fac_col[:], in_=fac.rearrange("o (c n m) -> n (o c) m", n=P, m=PACK))
-        load_scale_rows(nc.sync, wa_s, wa_scales, 1)
-        nc.scalar.dma_start(out=wa_c[:].bitcast(I32), in_=wa_words[0].bitcast(I32))
-        nc.sync.dma_start(out=xq_c[:].bitcast(I32), in_=xq_words[0].bitcast(I32))
-        load_scale_rows(nc.scalar, wa_s, wa_scales, 2)
+        load_scale_rows(nc.sync, wa_s, wa_scales, 0)
+        load_scale_rows(nc.scalar, wa_s, wa_scales, 1)
+        nc.sync.dma_start(out=wa_c[:].bitcast(I32), in_=wa_words[0].bitcast(I32))
         for q in range(4):
-            load_scale_rows(nc.scalar if q % 2 else nc.sync, xq_s, xq_scales, q)
-        load_scale_rows(nc.sync, wa_s, wa_scales, 3)
+            load_scale_rows(nc.scalar, xq_s, xq_scales, q)
+        nc.sync.dma_start(out=xq_c[:].bitcast(I32), in_=xq_words[0].bitcast(I32))
+        for q in range(2, 4):
+            load_scale_rows(nc.sync, wa_s, wa_scales, q)
         for c in range(2):
             nc.sync.dma_start(out=raw[c][:], in_=xf_rows[:, :, CHUNKS[c][0] : CHUNKS[c][1]])
         nc.sync.dma_start(out=wf_c[:].bitcast(I32), in_=wf_words[0].rearrange("p n t -> p (n t)").bitcast(I32))
@@ -93,7 +92,7 @@ def tile_list_token_overrides_kernel(tc, xq_words, xq_scales, wa_words, wa_scale
             lo, hi = CHUNKS[c]
             w = hi - lo
             grouped = keep.tile([P, w, PACK], BF16, name="grouped%d" % c, tag="stage%d" % c, align_bytes=64)
-            codes = keep.tile([P, w], U32, name="codes%d" % c, align_bytes=64)
+            codes = keep.tile([P, w], U32, name="codes%d" % c, tag="stage3" if c == 2 else "codes%d" % c, align_bytes=64)
             scales = keep.tile([P, w], U8, name="scales%d" % c, align_bytes=64)
             dst = grouped[:].rearrange("p (g i) t -> p g t i", i=4)
             src = raw[c][:].rearrange("p t (g i) -> p g t i", i=4)
@@ -108,7 +107,7 @@ def tile_list_token_overrides_kernel(tc, xq_words, xq_scales, wa_words, wa_scale
             lo, hi = CHUNKS[c]
             w = hi - lo
             codes, scales = operand
-            acc = psum.tile([P, BANK], F32, name="prod", tag="prod", bufs=2)
+            acc = psum.tile([P, BANK], F32, name="prod", tag="prod", bufs=4)
             nc.tensor.matmul_mx(
                 out=acc[:, :w],
                 lhsT=wf_c[:, P * b : P * (b + 1)].bitcast(FP8X4),
@@ -118,10 +117,14 @@ def tile_list_token_overrides_kernel(tc, xq_words, xq_scales, wa_words, wa_scale
                 start=True,
                 stop=True,
             )
-            nc.scalar.copy(out=p_sb[b][:, lo:hi], in_=acc[:, :w])
+            return acc[:, :w]
 
-        def spread_fac(c):
-            acc = psum.tile([P, PACK, P], F32, name="turn", tag="turn", bufs=2)
+        def p_out(c, b, acc):
+            lo, hi = CHUNKS[c]
+            nc.scalar.copy(out=p_sb[b][:, lo:hi], in_=acc)
+
+        def spread_fac(c, tag, bufs):
+            acc = psum.tile([P, PACK, P], F32, name="fac_acc", tag=tag, bufs=bufs)
             for m in range(PACK):
                 nc.tensor.transpose(acc[:, m, :], neg_col[:, c, m : m + 1].to_broadcast([P, P]), ident[:])
             nc.scalar.copy(
@@ -129,47 +132,69 @@ def tile_list_token_overrides_kernel(tc, xq_words, xq_scales, wa_words, wa_scale
                 in_=acc[:].rearrange("p m n -> p n m"),
             )
 
-        def override(b, lo, hi, slot):
-            listed = offsets[:, lo // GROUP : hi // GROUP]
-            diff = keep.tile([P, hi - lo], F32, name="diff%d_%d" % (b, lo), tag=slot, align_bytes=64)
-            nc.vector.tensor_tensor(diff[:], z[b][:].indirect(listed), p_sb[b][:, lo:hi], ALU.subtract)
-            nc.vector.tensor_tensor(page[b][:].indirect(listed), diff[:], neg_fac[:, lo:hi], ALU.mult)
+        def listed(lo, hi):
+            return offsets[:, lo // GROUP : hi // GROUP]
 
+        def gather(b, lo, hi, diff):
+            nc.vector.tensor_tensor(diff, z[b][:].indirect(listed(lo, hi)), p_sb[b][:, lo:hi], ALU.subtract)
+
+        def scatter(b, lo, hi, diff):
+            nc.vector.tensor_tensor(page[b][:].indirect(listed(lo, hi)), diff, neg_fac[:, lo:hi], ALU.mult)
+
+        def override(b, lo, hi, slot):
+            diff = keep.tile([P, hi - lo], F32, name="diff%d_%d" % (b, lo), tag=slot, align_bytes=64)
+            gather(b, lo, hi, diff[:])
+            scatter(b, lo, hi, diff[:])
+
+        nc.gpsimd.tensor_scalar(neg_col[:], fac_col[:], -1.0, 0.0, ALU.mult, ALU.add)
         z_block(0, "wide", 4)
         operands = [quantise(0), quantise(1)]
-        nc.gpsimd.tensor_scalar(neg_col[:], fac_col[:], -1.0, 0.0, ALU.mult, ALU.add)
-        p_block(0, 0, operands[0])
-        spread_fac(0)
-        p_block(1, 0, operands[1])
-        override(0, *CHUNKS[0], "stage1")
-        override(0, *CHUNKS[1], "diff")
-        z_block(1, "prod", 2)
-        p_block(0, 1, operands[0])
-        p_block(1, 1, operands[1])
-        override(1, *SECOND[0], "stage0")
-        for c in range(2, len(CHUNKS)):
-            spread_fac(c - 1)
-            operand = quantise(c)
-            override(1, *SECOND[c - 1], "stage%d" % c)
-            p_block(c, 0, operand)
-            override(0, *CHUNKS[c], "diff")
-            p_block(c, 1, operand)
-        override(1, *SECOND[-1], "diff")
+        for b in range(2):
+            for c in range(2):
+                p_out(c, b, p_block(c, b, operands[c]))
+        spread_fac(0, "prod", 4)
+        head = keep.tile([P, BANK], F32, name="head", tag="stage1", align_bytes=64)
+        for lo, hi in CHUNKS[:2]:
+            gather(0, lo, hi, head[:, lo:hi])
+        scatter(0, 0, BANK, head[:])
+        z_block(1, "prod", 4)
+        override(1, *CHUNKS[0], "stage0")
+        operands.append(quantise(2))
+        override(1, *CHUNKS[1], "stage2")
+        spread_fac(1, "prod", 4)
+        sums = [p_block(2, b, operands[2]) for b in range(2)]
+        p_out(2, 0, sums[0])
+        override(0, 512, 768, "diff")
+        operands.append(quantise(3))
+        p_out(2, 1, sums[1])
+        override(0, 768, 1024, "stage3")
+        spread_fac(2, "prod", 4)
+        for b in range(2):
+            p_out(3, b, p_block(3, b, operands[3]))
+        override(0, *CHUNKS[3], "diff")
+        override(1, BANK, J, "diff")
 
         for c in range(T // BANK):
-            summed = psum.tile([P, PACK, P], F32, name="summed", tag="wide", bufs=4)
-            for i in range(PACK):
-                cols = slice(BANK * c + P * i, BANK * c + P * (i + 1))
-                nc.tensor.matmul(summed[:, i, :], z[0][:, cols], ident[:], start=True, stop=False, is_transpose=True)
-                nc.tensor.matmul(summed[:, i, :], page[0][:, cols], ident[:], start=False, stop=True, is_transpose=True)
+            summed = psum.tile([P, PACK, P], F32, name="summed", tag="prod", bufs=4)
+            for term, source in enumerate((z[0], page[0])):
+                for i in range(PACK):
+                    cols = slice(BANK * c + P * i, BANK * c + P * (i + 1))
+                    nc.tensor.matmul(
+                        summed[:, i, :],
+                        source[:, cols],
+                        ident[:],
+                        start=(term == 0 and i == 0),
+                        stop=(term == 1 and i == PACK - 1),
+                        is_transpose=True,
+                    )
             turned = ring.tile([P, PACK, P], F32, name="turned")
             nc.scalar.copy(out=turned[:], in_=summed[:])
-            back = psum.tile([P, PACK, P], F32, name="back", tag="turn", bufs=2)
+            back = psum.tile([P, PACK, P], F32, name="back", tag="wide", bufs=4)
             for i in range(PACK):
                 nc.tensor.transpose(back[:, i, :], turned[:, i, :], ident[:])
             done = keep.tile([P, BANK], F32, name="done%d" % c)
             nc.scalar.copy(out=done[:], in_=back[:].rearrange("p i n -> p (i n)"))
-            nc.sync.dma_start(out=out[0:P, BANK * c : BANK * (c + 1)], in_=done[:])
+            nc.scalar.dma_start(out=out[0:P, BANK * c : BANK * (c + 1)], in_=done[:])
 
         for lo, hi in TAIL:
             last = keep.tile([P, hi - lo], F32, name="last%d" % lo)

from contextlib import ExitStack

import concourse.mybir as mybir
from concourse.masks import make_identity

K, T, J, N = 512, 2048, 1536, 256
FLOPS = 2 * K * N * (T + J)

F32 = mybir.dt.float32
BF16 = mybir.dt.bfloat16
I32 = mybir.dt.int32
U32 = mybir.dt.uint32
U16 = mybir.dt.uint16
U8 = mybir.dt.uint8
FP8X4 = mybir.dt.float8_e4m3fn_x4
FP4X4 = mybir.dt.float4_e2m1fn_x4
ALU = mybir.AluOpType

P = 128
PACK = 4
BANK = 512
GROUP = 16
CHUNKS = ((0, 256), (256, 512), (512, 1024), (1024, 1536))
TAIL = ((0, 256), (256, 768), (768, 1280), (1280, 1792), (1792, 2048))


def tile_list_token_overrides_kernel(tc, xq_words, xq_scales, wa_words, wa_scales, xf, wf_words, wf_scales, fac, offs, out):
    nc = tc.nc
    with ExitStack() as ctx:
        keep = ctx.enter_context(tc.tile_pool(name="keep", bufs=1))
        ring = ctx.enter_context(tc.tile_pool(name="ring", bufs=2))
        psum = ctx.enter_context(tc.psum_pool(name="psum", bufs=1))

        offsets = keep.tile([P, J // GROUP], U16, name="offsets")
        xq_c = keep.tile([P, 2 * T], U8, name="xq_c", tag="stage2", align_bytes=64)
        xq_s = keep.tile([P, T], U8, name="xq_s", align_bytes=64)
        wa_c = keep.tile([P, 2 * N], U8, name="wa_c", align_bytes=64)
        wa_s = keep.tile([P, N], U8, name="wa_s", align_bytes=64)
        wf_c = keep.tile([P, N], U32, name="wf_c", align_bytes=64)
        wf_s = keep.tile([P, N], U8, name="wf_s", align_bytes=64)
        fac_col = keep.tile([P, J // BANK, PACK], F32, name="fac_col")
        neg_col = keep.tile([P, J // BANK, PACK], F32, name="neg_col")
        neg_fac = keep.tile([P, J], F32, name="neg_fac")
        ident = keep.tile([P, P], F32, name="ident")
        z = [keep.tile([P, T], F32, name="z%d" % b) for b in range(2)]
        page = [keep.tile([P, T], F32, name="page%d" % b) for b in range(2)]
        p_sb = [keep.tile([P, J], F32, name="p%d" % b) for b in range(2)]
        raw = [keep.tile([P, PACK, hi - lo], F32, name="raw%d" % lo) for lo, hi in CHUNKS]

        def load_scale_rows(queue, plane, rows, q):
            queue.dma_start(out=plane[32 * q : 32 * q + 4, :].bitcast(I32), in_=rows[0, 4 * q : 4 * q + 4, :].bitcast(I32))

        xf_rows = xf.rearrange("(p t) j -> p t j", t=PACK)
        nc.gpsimd.dma_start(out=fac_col[:], in_=fac.rearrange("o (c n m) -> n (o c) m", n=P, m=PACK))
        load_scale_rows(nc.sync, wa_s, wa_scales, 0)
        load_scale_rows(nc.scalar, wa_s, wa_scales, 1)
        nc.sync.dma_start(out=wa_c[:].bitcast(I32), in_=wa_words[0].bitcast(I32))
        for q in range(4):
            load_scale_rows(nc.scalar, xq_s, xq_scales, q)
        nc.sync.dma_start(out=xq_c[:].bitcast(I32), in_=xq_words[0].bitcast(I32))
        for q in range(2, 4):
            load_scale_rows(nc.sync, wa_s, wa_scales, q)
        for c in range(2):
            nc.sync.dma_start(out=raw[c][:], in_=xf_rows[:, :, CHUNKS[c][0] : CHUNKS[c][1]])
        nc.sync.dma_start(out=wf_c[:].bitcast(I32), in_=wf_words[0].rearrange("p n t -> p (n t)").bitcast(I32))
        for q in range(4):
            load_scale_rows(nc.sync, wf_s, wf_scales, q)
        nc.sync.dma_start(out=offsets[:], in_=offs)
        for c in range(2, len(CHUNKS)):
            nc.sync.dma_start(out=raw[c][:], in_=xf_rows[:, :, CHUNKS[c][0] : CHUNKS[c][1]])

        nc.vector.memset(page[0][:, : T // 2 - 1], 0.0)
        nc.vector.memset(page[0][:, T // 2 - 1 :], 0.0)
        make_identity(nc, ident[:])
        nc.gpsimd.memset(page[1][:], 0.0)

        def z_block(b, tag, bufs):
            for c in range(T // BANK):
                acc = psum.tile([P, BANK], F32, name="z_acc", tag=tag, bufs=bufs)
                nc.tensor.matmul_mx(
                    out=acc[:],
                    lhsT=wa_c[:, 2 * P * b : 2 * P * (b + 1)].bitcast(FP4X4),
                    lhsT_scale=wa_s[:, P * b : P * (b + 1)],
                    rhs=xq_c[:, 2 * BANK * c : 2 * BANK * (c + 1)].bitcast(FP4X4),
                    rhs_scale=xq_s[:, BANK * c : BANK * (c + 1)],
                    start=True,
                    stop=True,
                )
                nc.scalar.copy(out=z[b][:, BANK * c : BANK * (c + 1)], in_=acc[:])

        def quantise(c):
            lo, hi = CHUNKS[c]
            w = hi - lo
            grouped = keep.tile([P, w, PACK], BF16, name="grouped%d" % c, tag="stage%d" % c, align_bytes=64)
            codes = keep.tile([P, w], U32, name="codes%d" % c, tag="stage3" if c == 2 else "codes%d" % c, align_bytes=64)
            scales = keep.tile([P, w], U8, name="scales%d" % c, align_bytes=64)
            dst = grouped[:].rearrange("p (g i) t -> p g t i", i=4)
            src = raw[c][:].rearrange("p t (g i) -> p g t i", i=4)
            if c < 2:
                nc.vector.tensor_copy(out=dst, in_=src)
            else:
                nc.scalar.copy(out=dst, in_=src)
            nc.vector.quantize_mx(out=codes[:].bitcast(FP8X4), scales=scales[:], in_=grouped[:].rearrange("p w t -> p (w t)"))
            return codes, scales

        def p_block(c, b, operand):
            lo, hi = CHUNKS[c]
            w = hi - lo
            codes, scales = operand
            acc = psum.tile([P, BANK], F32, name="prod", tag="prod", bufs=4)
            nc.tensor.matmul_mx(
                out=acc[:, :w],
                lhsT=wf_c[:, P * b : P * (b + 1)].bitcast(FP8X4),
                lhsT_scale=wf_s[:, P * b : P * (b + 1)],
                rhs=codes[:].bitcast(FP8X4),
                rhs_scale=scales[:],
                start=True,
                stop=True,
            )
            return acc[:, :w]

        def p_out(c, b, acc):
            lo, hi = CHUNKS[c]
            nc.scalar.copy(out=p_sb[b][:, lo:hi], in_=acc)

        def spread_fac(c, tag, bufs):
            acc = psum.tile([P, PACK, P], F32, name="fac_acc", tag=tag, bufs=bufs)
            for m in range(PACK):
                nc.tensor.transpose(acc[:, m, :], neg_col[:, c, m : m + 1].to_broadcast([P, P]), ident[:])
            nc.scalar.copy(
                out=neg_fac[:, BANK * c : BANK * (c + 1)].rearrange("p (n m) -> p n m", m=PACK),
                in_=acc[:].rearrange("p m n -> p n m"),
            )

        def listed(lo, hi):
            return offsets[:, lo // GROUP : hi // GROUP]

        def gather(b, lo, hi, diff):
            nc.vector.tensor_tensor(diff, z[b][:].indirect(listed(lo, hi)), p_sb[b][:, lo:hi], ALU.subtract)

        def scatter(b, lo, hi, diff):
            nc.vector.tensor_tensor(page[b][:].indirect(listed(lo, hi)), diff, neg_fac[:, lo:hi], ALU.mult)

        def override(b, lo, hi, slot):
            diff = keep.tile([P, hi - lo], F32, name="diff%d_%d" % (b, lo), tag=slot, align_bytes=64)
            gather(b, lo, hi, diff[:])
            scatter(b, lo, hi, diff[:])

        nc.gpsimd.tensor_scalar(neg_col[:], fac_col[:], -1.0, 0.0, ALU.mult, ALU.add)
        z_block(0, "wide", 4)
        operands = [quantise(0), quantise(1)]
        for b in range(2):
            for c in range(2):
                p_out(c, b, p_block(c, b, operands[c]))
        spread_fac(0, "prod", 4)
        head = keep.tile([P, BANK], F32, name="head", tag="stage1", align_bytes=64)
        for lo, hi in CHUNKS[:2]:
            gather(0, lo, hi, head[:, lo:hi])
        scatter(0, 0, BANK, head[:])
        z_block(1, "prod", 4)
        override(1, *CHUNKS[0], "stage0")
        operands.append(quantise(2))
        override(1, *CHUNKS[1], "stage2")
        spread_fac(1, "prod", 4)
        sums = [p_block(2, b, operands[2]) for b in range(2)]
        p_out(2, 0, sums[0])
        override(0, 512, 768, "diff")
        operands.append(quantise(3))
        p_out(2, 1, sums[1])
        override(0, 768, 1024, "stage3")
        spread_fac(2, "prod", 4)
        for b in range(2):
            p_out(3, b, p_block(3, b, operands[3]))
        override(0, *CHUNKS[3], "diff")
        override(1, BANK, J, "diff")

        for c in range(T // BANK):
            summed = psum.tile([P, PACK, P], F32, name="summed", tag="prod", bufs=4)
            for term, source in enumerate((z[0], page[0])):
                for i in range(PACK):
                    cols = slice(BANK * c + P * i, BANK * c + P * (i + 1))
                    nc.tensor.matmul(
                        summed[:, i, :],
                        source[:, cols],
                        ident[:],
                        start=(term == 0 and i == 0),
                        stop=(term == 1 and i == PACK - 1),
                        is_transpose=True,
                    )
            turned = ring.tile([P, PACK, P], F32, name="turned")
            nc.scalar.copy(out=turned[:], in_=summed[:])
            back = psum.tile([P, PACK, P], F32, name="back", tag="wide", bufs=4)
            for i in range(PACK):
                nc.tensor.transpose(back[:, i, :], turned[:, i, :], ident[:])
            done = keep.tile([P, BANK], F32, name="done%d" % c)
            nc.scalar.copy(out=done[:], in_=back[:].rearrange("p i n -> p (i n)"))
            nc.scalar.dma_start(out=out[0:P, BANK * c : BANK * (c + 1)], in_=done[:])

        for lo, hi in TAIL:
            last = keep.tile([P, hi - lo], F32, name="last%d" % lo)
            nc.vector.tensor_tensor(last[:], z[1][:, lo:hi], page[1][:, lo:hi], ALU.add)
            nc.sync.dma_start(out=out[P : 2 * P, lo:hi], in_=last[:])
